import numpy as np
import ml_dtypes

BF16 = ml_dtypes.bfloat16


def bf(x):
    return np.asarray(x, np.float32).astype(BF16)


def f32(x):
    return np.asarray(x, np.float32)


def f64(x):
    return np.asarray(x).astype(np.float64)


def striped(idx):
    return np.tile(idx.reshape(-1, 16).T, (8, 1))


S, K, N, V, D, H, O = 256, 128, 256, 128, 2, 256, 128


def gelu_tanh(v):
    return 0.5 * v * (1.0 + np.tanh(np.sqrt(2.0 / np.pi) * (v + 0.044715 * v**3)))


def setup_inputs():
    return {"table": bf(np.random.standard_normal((K, S))), "w": bf(np.random.standard_normal((D, K, H)) / np.sqrt(D * K)), "b": f32(0.5 * np.random.standard_normal((H, 1))), "w2": bf(np.random.standard_normal((H, O)) / np.sqrt(H)), "offs": striped(np.random.permutation(np.tile(np.arange(S), 2))[:N])}


def reference(table, w, b, w2, offs):
    idx = offs[:16].T.reshape(-1)
    x = f64(table)[:, idx]
    t = sum(f64(w)[d].T @ x[:, d * V : (d + 1) * V] for d in range(D)) + f64(b)
    t = gelu_tanh(t)
    return f64(w2).T @ t

@@ -1,0 +1,50 @@
+import concourse.mybir as mybir
+
+P = 128
+NODES, EDGES, ENDS, HIDDEN, OUTS = 256, 128, 2, 256, 128
+BLOCKS = HIDDEN // P
+LIST_ROWS = 16
+END_COLS = EDGES // LIST_ROWS
+
+FLOPS = 2 * ENDS * P * HIDDEN * EDGES + 2 * HIDDEN * OUTS * EDGES
+
+BF16, F32, U16 = mybir.dt.bfloat16, mybir.dt.float32, mybir.dt.uint16
+GELU = mybir.ActivationFunctionType.Gelu_apprx_tanh
+
+
+def tile_rows_edge2_gelu_rep_kernel(tc, table, w, b, w2, offs, out):
+    nc = tc.nc
+    with (
+        tc.tile_pool(name="sbuf", bufs=1) as sbuf,
+        tc.psum_pool(name="psum", bufs=1) as psum,
+    ):
+        offsets = sbuf.tile([P, ENDS * END_COLS], U16, name="offsets")
+        nodes = sbuf.tile([P, NODES], BF16, name="nodes")
+        layer1 = sbuf.tile([P, ENDS, HIDDEN], BF16, name="layer1")
+        bias = sbuf.tile([P, BLOCKS], F32, name="bias")
+        layer2 = sbuf.tile([P, BLOCKS, OUTS], BF16, name="layer2")
+
+        nc.sync.dma_start(offsets[:], offs)
+        nc.sync.dma_start(nodes[:], table)
+        nc.scalar.dma_start(layer1[:], w.rearrange("d k i -> k d i"))
+        nc.scalar.dma_start(bias[:], b.rearrange("(a p) o -> p (a o)", p=P))
+        nc.sync.dma_start(layer2[:], w2.rearrange("(a p) o -> p a o", p=P))
+
+        hidden = []
+        for a in range(BLOCKS):
+            pre = psum.tile([P, EDGES], F32, name=f"pre{a}")
+            for d in range(ENDS):
+                picked = nodes[:].indirect(offsets[:, d * END_COLS : (d + 1) * END_COLS])
+                nc.tensor.matmul(pre[:], layer1[:, d, a * P : (a + 1) * P], picked,
+                                 start=(d == 0), stop=(d == ENDS - 1))
+            h = sbuf.tile([P, EDGES], BF16, name=f"h{a}")
+            nc.scalar.activation(h[:], pre[:], GELU, bias=bias[:, a : a + 1])
+            hidden.append(h)
+
+        acc = psum.tile([OUTS, EDGES], F32, name="acc")
+        for a in range(BLOCKS):
+            nc.tensor.matmul(acc[:], layer2[:, a, :], hidden[a][:],
+                             start=(a == 0), stop=(a == BLOCKS - 1))
+        result = sbuf.tile([OUTS, EDGES], F32, name="result")
+        nc.vector.tensor_copy(result[:], acc[:])
+        nc.sync.dma_start(out, result[:])

@@ -30,6 +30,11 @@ def tile_rows_edge2_gelu_rep_kernel(tc, table, w, b, w2, offs, out):
         nc.scalar.dma_start(bias[:], b.rearrange("(a p) o -> p (a o)", p=P))
         nc.sync.dma_start(layer2[:], w2.rearrange("(a p) o -> p a o", p=P))
 
+        zero = sbuf.tile([P, 1], F32, name="zero")
+        unused = sbuf.tile([P, 1], F32, name="unused")
+        nc.vector.memset(zero[:], 0.0)
+        nc.scalar.activation(unused[:], zero[:], GELU, bias=zero[:])
+
         hidden = []
         for a in range(BLOCKS):
             pre = psum.tile([P, EDGES], F32, name=f"pre{a}")

@@ -20,31 +20,31 @@ def tile_rows_edge2_gelu_rep_kernel(tc, table, w, b, w2, offs, out):
     ):
         offsets = sbuf.tile([P, ENDS * END_COLS], U16, name="offsets")
         nodes = sbuf.tile([P, NODES], BF16, name="nodes")
-        layer1 = sbuf.tile([P, ENDS, HIDDEN], BF16, name="layer1")
+        layer1 = [sbuf.tile([P, HIDDEN], BF16, name=f"layer1_{d}") for d in range(ENDS)]
         bias = sbuf.tile([P, BLOCKS], F32, name="bias")
         layer2 = sbuf.tile([P, BLOCKS, OUTS], BF16, name="layer2")
 
-        nc.sync.dma_start(offsets[:], offs)
         nc.sync.dma_start(nodes[:], table)
-        nc.scalar.dma_start(layer1[:], w.rearrange("d k i -> k d i"))
-        nc.scalar.dma_start(bias[:], b.rearrange("(a p) o -> p (a o)", p=P))
-        nc.sync.dma_start(layer2[:], w2.rearrange("(a p) o -> p a o", p=P))
+        nc.scalar.dma_start(layer1[0][:], w[0])
+        nc.sync.dma_start(offsets[:], offs)
+        nc.sync.dma_start(layer1[1][:], w[1])
+        nc.scalar.dma_start(bias[:], b.rearrange("(p a) o -> p (a o)", p=P))
+        nc.sync.dma_start(layer2[:], w2.rearrange("(p a) o -> p a o", p=P))
 
         zero = sbuf.tile([P, 1], F32, name="zero")
         unused = sbuf.tile([P, 1], F32, name="unused")
         nc.vector.memset(zero[:], 0.0)
         nc.scalar.activation(unused[:], zero[:], GELU, bias=zero[:])
 
-        hidden = []
-        for a in range(BLOCKS):
-            pre = psum.tile([P, EDGES], F32, name=f"pre{a}")
-            for d in range(ENDS):
-                picked = nodes[:].indirect(offsets[:, d * END_COLS : (d + 1) * END_COLS])
-                nc.tensor.matmul(pre[:], layer1[:, d, a * P : (a + 1) * P], picked,
+        pre = [psum.tile([P, EDGES], F32, name=f"pre{a}") for a in range(BLOCKS)]
+        for d in range(ENDS):
+            picked = nodes[:].indirect(offsets[:, d * END_COLS : (d + 1) * END_COLS])
+            for a in range(BLOCKS):
+                nc.tensor.matmul(pre[a][:], layer1[d][:, a::BLOCKS], picked,
                                  start=(d == 0), stop=(d == ENDS - 1))
-            h = sbuf.tile([P, EDGES], BF16, name=f"h{a}")
-            nc.scalar.activation(h[:], pre[:], GELU, bias=bias[:, a : a + 1])
-            hidden.append(h)
+        hidden = [sbuf.tile([P, EDGES], BF16, name=f"h{a}") for a in range(BLOCKS)]
+        for a in range(BLOCKS):
+            nc.scalar.activation(hidden[a][:], pre[a][:], GELU, bias=bias[:, a : a + 1])
 
         acc = psum.tile([OUTS, EDGES], F32, name="acc")
         for a in range(BLOCKS):

import concourse.mybir as mybir

P = 128
NODES, EDGES, ENDS, HIDDEN, OUTS = 256, 128, 2, 256, 128
BLOCKS = HIDDEN // P
LIST_ROWS = 16
END_COLS = EDGES // LIST_ROWS

FLOPS = 2 * ENDS * P * HIDDEN * EDGES + 2 * HIDDEN * OUTS * EDGES

BF16, F32, U16 = mybir.dt.bfloat16, mybir.dt.float32, mybir.dt.uint16
GELU = mybir.ActivationFunctionType.Gelu_apprx_tanh


def tile_rows_edge2_gelu_rep_kernel(tc, table, w, b, w2, offs, out):
    nc = tc.nc
    with (
        tc.tile_pool(name="sbuf", bufs=1) as sbuf,
        tc.psum_pool(name="psum", bufs=1) as psum,
    ):
        offsets = sbuf.tile([P, ENDS * END_COLS], U16, name="offsets")
        nodes = sbuf.tile([P, NODES], BF16, name="nodes")
        layer1 = [sbuf.tile([P, HIDDEN], BF16, name=f"layer1_{d}") for d in range(ENDS)]
        bias = sbuf.tile([P, BLOCKS], F32, name="bias")
        layer2 = sbuf.tile([P, BLOCKS, OUTS], BF16, name="layer2")

        nc.sync.dma_start(nodes[:], table)
        nc.scalar.dma_start(layer1[0][:], w[0])
        nc.sync.dma_start(offsets[:], offs)
        nc.sync.dma_start(layer1[1][:], w[1])
        nc.scalar.dma_start(bias[:], b.rearrange("(p a) o -> p (a o)", p=P))
        nc.sync.dma_start(layer2[:], w2.rearrange("(p a) o -> p a o", p=P))

        zero = sbuf.tile([P, 1], F32, name="zero")
        unused = sbuf.tile([P, 1], F32, name="unused")
        nc.vector.memset(zero[:], 0.0)
        nc.scalar.activation(unused[:], zero[:], GELU, bias=zero[:])

        pre = [psum.tile([P, EDGES], F32, name=f"pre{a}") for a in range(BLOCKS)]
        for d in range(ENDS):
            picked = nodes[:].indirect(offsets[:, d * END_COLS : (d + 1) * END_COLS])
            for a in range(BLOCKS):
                nc.tensor.matmul(pre[a][:], layer1[d][:, a::BLOCKS], picked,
                                 start=(d == 0), stop=(d == ENDS - 1))
        hidden = [sbuf.tile([P, EDGES], BF16, name=f"h{a}") for a in range(BLOCKS)]
        for a in range(BLOCKS):
            nc.scalar.activation(hidden[a][:], pre[a][:], GELU, bias=bias[:, a : a + 1])

        acc = psum.tile([OUTS, EDGES], F32, name="acc")
        for a in range(BLOCKS):
            nc.tensor.matmul(acc[:], layer2[:, a, :], hidden[a][:],
                             start=(a == 0), stop=(a == BLOCKS - 1))
        result = sbuf.tile([OUTS, EDGES], F32, name="result")
        nc.vector.tensor_copy(result[:], acc[:])
        nc.sync.dma_start(out, result[:])
